import numpy as np
import ml_dtypes


def mxq(x, axis, fmt="e4m3"):
    dtype, down = {"e4m3": (ml_dtypes.float8_e4m3fn, 7), "e5m2": (ml_dtypes.float8_e5m2, 14)}[fmt]
    v = np.moveaxis(np.asarray(x, np.float32).astype(ml_dtypes.bfloat16).astype(np.float64), axis, -1)
    blocks = v.reshape(v.shape[:-1] + (-1, 32))
    amax = np.abs(blocks).max(-1, keepdims=True)
    byte = np.maximum(np.where(amax > 0, np.frexp(amax)[1] - 1 + 127, 0) - down, 1)
    scale = np.exp2(byte - 127.0)
    codes = (blocks / scale).astype(np.float32).astype(dtype).astype(np.float64)
    return np.moveaxis((codes * scale).reshape(v.shape), -1, axis)


WIDE = False


def mx_kscale(k):
    if not WIDE:
        return np.ones(k)
    levels = np.array([10, -10, 5, -5, 0])
    if k % 512:
        return np.exp2(np.random.permutation(np.resize(levels, k // 32))).repeat(32)
    a = np.empty((k // 512, 16))
    for p in range(k // 512):
        a[p, :8] = np.random.permutation(np.resize(levels, 8))
        for g in range(8):
            far = levels[np.abs(levels - a[p, g]) >= 10]
            a[p, g + 8] = far[np.random.randint(len(far))]
    return np.exp2(a.ravel()).repeat(32)


def f64(x):
    return np.asarray(x).astype(np.float64)


def striped(idx):
    return np.tile(np.asarray(idx).reshape(-1, 16).T, (8, 1)).astype(np.uint16)


def unstriped(offs):
    return offs[:16].T.reshape(-1).astype(np.int64)


E2M1 = np.array([0.0, 0.5, 1.0, 1.5, 2.0, 3.0, 4.0, 6.0, -0.0, -0.5, -1.0, -1.5, -2.0, -3.0, -4.0, -6.0])


def pack_weight(w, fmt):
    k, n = w.shape
    w = f64(np.asarray(w, np.float32).astype(ml_dtypes.bfloat16)).reshape(k // 32, 32, n)
    amax = np.abs(w).max(1)
    if fmt == "e4m3":
        byte = np.frexp(amax)[1] - 1 + 127 - 7
    else:
        mant, ex = np.frexp(amax / 6.0)
        byte = np.where(mant > 0.5, ex, ex - 1) + 127
    byte = np.clip(np.where(amax > 0, byte, 1), 1, 254)
    scaled = (w * np.exp2(127.0 - byte)[:, None, :]).reshape(k, n).astype(np.float32)
    by_word = np.ascontiguousarray(scaled.reshape(k // 512, 128, 4, n).transpose(0, 1, 3, 2))
    if fmt == "e4m3":
        words = by_word.astype(ml_dtypes.float8_e4m3fn).view(np.uint8)
    else:
        c = by_word.astype(ml_dtypes.float4_e2m1fn).view(np.uint8) & 0xF
        words = (c[..., 0::2] | (c[..., 1::2] << 4)).reshape(k // 512, 128, 2 * n)
    return np.ascontiguousarray(words), np.ascontiguousarray(byte.astype(np.uint8).reshape(k // 512, 16, n))


def unpack_weight(words, scales, fmt):
    g, _, n = scales.shape
    words = np.ascontiguousarray(words).reshape(g, 128, n, -1)
    if fmt == "e4m3":
        vals = words.view(ml_dtypes.float8_e4m3fn).astype(np.float64)
    else:
        nib = np.empty((g, 128, n, 4), np.uint8)
        nib[..., 0::2] = words & 0xF
        nib[..., 1::2] = words >> 4
        vals = E2M1[nib]
    vals = vals * np.repeat(np.exp2(scales.astype(np.float64) - 127.0), 8, axis=1)[..., None]
    return vals.transpose(0, 1, 3, 2).reshape(g * 512, n)


D, E, T, I, G, U, Q = 512, 512, 2048, 512, 64, 512, 128


def setup_inputs():
    n = np.random.standard_normal
    idx = np.random.permutation(T)[:I]
    idx2 = np.random.permutation(U)[:G]
    fd = mx_kscale(D)
    fe = mx_kscale(E)
    pgsump = pack_weight(n((D, U)) / fd[:, None], "e2m1")
    keysp = pack_weight(n((D, T)) / fd[:, None], "e2m1")
    valsp = pack_weight(n((E, T)) / fe[:, None], "e2m1")
    return {
        "pquery": (n((D, Q)) * 1.0 / np.sqrt(D) * fd[:, None]).astype(np.float32),
        "pgsum_words": pgsump[0],
        "pgsum_scales": pgsump[1],
        "query": (n((D, Q)) * 0.7 / np.sqrt(D) * fd[:, None]).astype(np.float32),
        "keys_words": keysp[0],
        "keys_scales": keysp[1],
        "even": (np.random.uniform(0.1, 0.6, (Q, 1))).astype(np.float32),
        "gout": (n((E, Q)) * 1 / np.sqrt(E) * fe[:, None]).astype(np.float32),
        "vals_words": valsp[0],
        "vals_scales": valsp[1],
        "dquery": (n((D, Q)) * 1.0 / np.sqrt(D) * fd[:, None]).astype(np.float32),
        "base": (0.5 * n((Q, I))).astype(np.float32),
        "offs": striped(idx),
        "offs2": striped(idx2),
    }


def reference(pquery, pgsum_words, pgsum_scales, query, keys_words, keys_scales, even, gout, vals_words, vals_scales, dquery, base, offs, offs2):
    idx = unstriped(offs)
    idx2 = unstriped(offs2)
    pgsumu = unpack_weight(pgsum_words, pgsum_scales, "e2m1")
    keysu = unpack_weight(keys_words, keys_scales, "e2m1")
    valsu = unpack_weight(vals_words, vals_scales, "e2m1")
    pqueryq = mxq(f64(pquery), 0, "e4m3")
    pgsumidx2g = pgsumu[:, idx2]
    b = pqueryq.T @ pgsumidx2g
    pb = np.exp(b - np.max(b, axis=1, keepdims=True))
    zb = np.sum(pb, axis=1, keepdims=True)
    queryq = mxq(f64(query), 0, "e4m3")
    keysidxg = keysu[:, idx]
    a = queryq.T @ keysidxg
    dqueryq = mxq(f64(dquery), 0, "e4m3")
    ta = dqueryq.T @ keysidxg
    pa = np.exp(a)
    s = pa.reshape(Q, G, I // G).sum(axis=2)
    goutq = mxq(f64(gout), 0, "e4m3")
    valsidxg = valsu[:, idx]
    c0 = goutq.T @ valsidxg
    w = pb / zb * (1.0 - f64(even)) + f64(even) / 64.0
    e1 = w / s
    r1 = np.repeat(e1, I // G, axis=1)
    ds = w * (pa * c0).reshape(Q, G, I // G).sum(axis=2) / np.square(s) * (-1.0)
    r2 = np.repeat(ds, I // G, axis=1)
    dpa = r1 * c0 + r2
    xpa = ta * pa
    xs = xpa.reshape(Q, G, I // G).sum(axis=2)
    xe1 = xs * w / np.square(s) * (-1.0)
    xr1 = np.repeat(xe1, I // G, axis=1)
    xds = ((xpa * c0).reshape(Q, G, I // G).sum(axis=2) * w - xs * s * 2.0 * w * (pa * c0).reshape(Q, G, I // G).sum(axis=2) / np.square(s)) / np.square(s) * (-1.0)
    xr2 = np.repeat(xds, I // G, axis=1)
    xdpa = xr1 * c0 + xr2
    xda = xdpa * pa + xpa * dpa
    y = xda * 512.0 + f64(base)
    return y

@@ -1,0 +1,195 @@
+from contextlib import ExitStack
+
+import concourse.mybir as mybir
+
+D, E, T, I, G, U, Q = 512, 512, 2048, 512, 64, 512, 128
+R = I // G
+P = 128
+PACK = 4
+FLOPS = 2 * Q * (2 * D * I + E * I + D * G)
+
+F32 = mybir.dt.float32
+BF16 = mybir.dt.bfloat16
+I32 = mybir.dt.int32
+U32 = mybir.dt.uint32
+U16 = mybir.dt.uint16
+U8 = mybir.dt.uint8
+FP8X4 = mybir.dt.float8_e4m3fn_x4
+FP4X4 = mybir.dt.float4_e2m1fn_x4
+ALU = mybir.AluOpType
+ACT = mybir.ActivationFunctionType
+AX = mybir.AxisListType
+
+
+def tile_attend_hvevenmass_a_kernel(tc, pquery, pgsum_words, pgsum_scales, query, keys_words, keys_scales, even, gout,
+                                     vals_words, vals_scales, dquery, base, offs, offs2, out):
+    nc = tc.nc
+    with ExitStack() as ctx:
+        lists = ctx.enter_context(tc.tile_pool(name="lists", bufs=1))
+        sb = ctx.enter_context(tc.tile_pool(name="sb", bufs=1))
+        psum = ctx.enter_context(tc.psum_pool(name="psum", bufs=1))
+
+        token_list = lists.tile([P, I // 16], U16, name="token_list")
+        page_list = lists.tile([P, G // 16], U16, name="page_list")
+
+        def words_tile(name, cols):
+            return sb.tile([P, cols], U16, name=name, align_bytes=64)
+
+        def scales_tile(name, cols):
+            return sb.tile([P, cols], U8, name=name, align_bytes=64)
+
+        def load_words(tile, words):
+            nc.sync.dma_start(out=tile[:].bitcast(I32), in_=words[0].bitcast(I32))
+
+        def load_scales(tile, scales):
+            for quad in range(4):
+                nc.sync.dma_start(out=tile[32 * quad:32 * quad + 4, :].bitcast(I32),
+                                  in_=scales[0, 4 * quad:4 * quad + 4, :].bitcast(I32))
+
+        def load_rows(name, rows):
+            raw = sb.tile([P, PACK, Q], F32, name=name + "_raw")
+            nc.sync.dma_start(out=raw[:], in_=rows.rearrange("(p j) q -> p j q", j=PACK))
+            return raw
+
+        def interleave(name, raw):
+            grouped = sb.tile([P, Q, PACK], BF16, name=name + "_bf", align_bytes=64)
+            nc.scalar.activation(out=grouped[:], in_=raw[:].rearrange("p j q -> p q j"), func=ACT.Copy)
+            return grouped
+
+        def quantize(name, grouped):
+            codes = sb.tile([P, Q], U32, name=name + "_codes", align_bytes=64)
+            scales = sb.tile([P, Q], U8, name=name + "_scales", align_bytes=64)
+            nc.vector.quantize_mx(out=codes[:].bitcast(FP8X4), scales=scales[:],
+                                  in_=grouped[:].rearrange("p q j -> p (q j)"))
+            return codes, scales
+
+        def gather(name, window, offsets, cols, dtype):
+            picked = sb.tile([P, cols], dtype, name=name, align_bytes=64)
+            nc.vector.tensor_copy(out=picked[:], in_=window[:].indirect(offsets[:]))
+            return picked
+
+        def product(name, rows, words, scales, cols):
+            acc = psum.tile([P, cols], F32, name=name)
+            nc.tensor.matmul_mx(out=acc[:], lhsT=rows[0][:].bitcast(FP8X4), lhsT_scale=rows[1][:],
+                                rhs=words[:].bitcast(FP4X4), rhs_scale=scales[:], start=True, stop=True)
+            return acc
+
+        key_words, key_scales = words_tile("key_words", T), scales_tile("key_scales", T)
+        val_words, val_scales = words_tile("val_words", T), scales_tile("val_scales", T)
+        page_words, page_scales = words_tile("page_words", U), scales_tile("page_scales", U)
+        nc.vector.memset(key_scales[:].bitcast(I32), 0)
+        nc.gpsimd.memset(val_scales[:].bitcast(I32), 0)
+        nc.gpsimd.memset(page_scales[:].bitcast(I32), 0)
+
+        nc.sync.dma_start(token_list[:], offs)
+        load_words(key_words, keys_words)
+        load_scales(key_scales, keys_scales)
+        q_raw = load_rows("q", query)
+        dq_raw = load_rows("dq", dquery)
+        load_words(val_words, vals_words)
+        load_scales(val_scales, vals_scales)
+        g_raw = load_rows("g", gout)
+        nc.sync.dma_start(page_list[:], offs2)
+        load_words(page_words, pgsum_words)
+        load_scales(page_scales, pgsum_scales)
+        pq_raw = load_rows("pq", pquery)
+        even_t = sb.tile([P, 1], F32, name="even_t")
+        nc.sync.dma_start(out=even_t[:], in_=even)
+        base_t = sb.tile([P, I], F32, name="base_t")
+        nc.sync.dma_start(out=base_t[:], in_=base)
+
+        q_bf = interleave("q", q_raw)
+        dq_bf = interleave("dq", dq_raw)
+        kw = gather("kw", key_words, token_list, I, U16)
+        ks = gather("ks", key_scales, token_list, I, U8)
+        q_mx = quantize("q", q_bf)
+        a = product("a", q_mx, kw, ks, I)
+        dq_mx = quantize("dq", dq_bf)
+        ta = product("ta", dq_mx, kw, ks, I)
+        pa = sb.tile([P, I], F32, name="pa")
+        nc.scalar.activation(out=pa[:], in_=a[:], func=ACT.Exp)
+
+        g_bf = interleave("g", g_raw)
+        pq_bf = interleave("pq", pq_raw)
+        vw = gather("vw", val_words, token_list, I, U16)
+        vs = gather("vs", val_scales, token_list, I, U8)
+        g_mx = quantize("g", g_bf)
+        c0 = product("c0", g_mx, vw, vs, I)
+
+        pw = gather("pw", page_words, page_list, G, U16)
+        ps = gather("ps", page_scales, page_list, G, U8)
+        pq_mx = quantize("pq", pq_bf)
+        b = product("b", pq_mx, pw, ps, G)
+
+        def big(name):
+            return sb.tile([P, I], F32, name=name)
+
+        def small(name, cols=G):
+            return sb.tile([P, cols], F32, name=name)
+
+        def paged(ap):
+            return ap.rearrange("p (g r) -> p g r", r=R)
+
+        def spread(ap):
+            return ap.unsqueeze(2).to_broadcast([P, ap.shape[1], R])
+
+        def page_sum(dst, src):
+            nc.vector.tensor_reduce(out=dst, in_=paged(src), axis=AX.X, op=ALU.add)
+
+        s = small("s")
+        page_sum(s[:], pa[:])
+        xpa = big("xpa")
+        nc.vector.tensor_tensor(out=xpa[:], in0=ta[:], in1=pa[:], op=ALU.mult)
+        neg_max = small("neg_max", 1)
+        nc.vector.tensor_reduce(out=neg_max[:], in_=b[:], axis=AX.X, op=ALU.max, negate=True)
+        pb = small("pb")
+        zb = small("zb", 1)
+        nc.scalar.activation(out=pb[:], in_=b[:], func=ACT.Exp, bias=neg_max[:], accum_out=zb[:])
+        rest = small("rest", 1)
+        nc.scalar.activation(out=rest[:], in_=even_t[:], func=ACT.Copy, scale=-512.0, bias=512.0)
+        floor = small("floor", 1)
+        nc.scalar.activation(out=floor[:], in_=even_t[:], func=ACT.Copy, scale=512.0 / G)
+        rs = small("rs")
+        nc.vector.reciprocal(out=rs[:], in_=s[:])
+        xs = small("xs")
+        page_sum(xs[:], xpa[:])
+        rz = small("rz", 1)
+        nc.vector.reciprocal(out=rz[:], in_=zb[:])
+        pc = big("pc")
+        nc.vector.tensor_tensor(out=pc[:], in0=c0[:], in1=pa[:], op=ALU.mult)
+        tbar = small("tbar")
+        nc.vector.tensor_tensor(out=tbar[:], in0=xs[:], in1=rs[:], op=ALU.mult)
+        share = small("share", 1)
+        nc.scalar.activation(out=share[:], in_=rz[:], func=ACT.Copy, scale=rest[:])
+        w = small("w")
+        nc.scalar.activation(out=w[:], in_=pb[:], func=ACT.Identity, scale=share[:], bias=floor[:])
+        pcs = small("pcs")
+        page_sum(pcs[:], pc[:])
+        u = big("u")
+        nc.vector.tensor_tensor(out=paged(u[:]), in0=paged(ta[:]), in1=spread(tbar[:]), op=ALU.subtract)
+        cbar = small("cbar")
+        nc.vector.tensor_tensor(out=cbar[:], in0=pcs[:], in1=rs[:], op=ALU.mult)
+        ws = small("ws")
+        nc.vector.tensor_tensor(out=ws[:], in0=w[:], in1=rs[:], op=ALU.mult)
+        pu = big("pu")
+        nc.vector.tensor_tensor(out=pu[:], in0=pa[:], in1=u[:], op=ALU.mult)
+        v = big("v")
+        nc.vector.tensor_tensor(out=paged(v[:]), in0=paged(c0[:]), in1=spread(cbar[:]), op=ALU.subtract)
+        y = big("y")
+        nc.vector.tensor_tensor(out=paged(y[:]), in0=paged(pu[:]), in1=spread(ws[:]), op=ALU.mult)
+
+        yv, pcov, diff, res = big("yv"), big("pcov"), big("diff"), big("res")
+        dsum, cov = small("dsum"), small("cov")
+        halves = [(slice(h * I // 2, (h + 1) * I // 2), slice(h * G // 2, (h + 1) * G // 2)) for h in range(2)]
+        for cols, pages in halves:
+            nc.vector.tensor_tensor(out=yv[:, cols], in0=y[:, cols], in1=v[:, cols], op=ALU.mult)
+        for cols, pages in halves:
+            page_sum(dsum[:, pages], yv[:, cols])
+        for cols, pages in halves:
+            nc.vector.tensor_tensor(out=diff[:, cols], in0=yv[:, cols], in1=base_t[:, cols], op=ALU.add)
+            nc.vector.tensor_tensor(out=cov[:, pages], in0=dsum[:, pages], in1=rs[:, pages], op=ALU.mult)
+        for cols, pages in halves:
+            nc.vector.tensor_tensor(out=paged(pcov[:, cols]), in0=paged(pa[:, cols]), in1=spread(cov[:, pages]), op=ALU.mult)
+        for cols, pages in halves:
+            nc.vector.tensor_tensor(out=res[:, cols], in0=diff[:, cols], in1=pcov[:, cols], op=ALU.subtract)
+            nc.sync.dma_start(out=out[:, cols], in_=res[:, cols])

@@ -33,44 +33,41 @@ def tile_attend_hvevenmass_a_kernel(tc, pquery, pgsum_words, pgsum_scales, query
         page_list = lists.tile([P, G // 16], U16, name="page_list")
 
         def words_tile(name, cols):
-            return sb.tile([P, cols], U16, name=name, align_bytes=64)
+            return sb.tile([P, cols], U16, name=name, tag=name, align_bytes=64)
 
         def scales_tile(name, cols):
-            return sb.tile([P, cols], U8, name=name, align_bytes=64)
+            return sb.tile([P, cols], U8, name=name, tag=name, align_bytes=64)
 
         def load_words(tile, words):
             nc.sync.dma_start(out=tile[:].bitcast(I32), in_=words[0].bitcast(I32))
 
         def load_scales(tile, scales):
-            for quad in range(4):
-                nc.sync.dma_start(out=tile[32 * quad:32 * quad + 4, :].bitcast(I32),
-                                  in_=scales[0, 4 * quad:4 * quad + 4, :].bitcast(I32))
+            for row in range(4):
+                nc.sync.dma_start(out=tile[row:P:32, :].bitcast(I32), in_=scales[0, row:16:4, :].bitcast(I32))
 
         def load_rows(name, rows):
             raw = sb.tile([P, PACK, Q], F32, name=name + "_raw")
             nc.sync.dma_start(out=raw[:], in_=rows.rearrange("(p j) q -> p j q", j=PACK))
             return raw
 
-        def interleave(name, raw):
-            grouped = sb.tile([P, Q, PACK], BF16, name=name + "_bf", align_bytes=64)
-            nc.scalar.activation(out=grouped[:], in_=raw[:].rearrange("p j q -> p q j"), func=ACT.Copy)
-            return grouped
+        def interleave(grouped, raw):
+            nc.scalar.activation(out=grouped, in_=raw[:].rearrange("p j q -> p q j"), func=ACT.Copy)
 
-        def quantize(name, grouped):
-            codes = sb.tile([P, Q], U32, name=name + "_codes", align_bytes=64)
-            scales = sb.tile([P, Q], U8, name=name + "_scales", align_bytes=64)
+        def quantize(name, grouped, tags):
+            codes = sb.tile([P, 2 * Q], U32, name=name + "_codes", tag=tags[0], align_bytes=64)
+            scales = sb.tile([P, 2 * Q], U8, name=name + "_scales", tag=tags[1], align_bytes=64)
             nc.vector.quantize_mx(out=codes[:].bitcast(FP8X4), scales=scales[:],
-                                  in_=grouped[:].rearrange("p q j -> p (q j)"))
-            return codes, scales
+                                  in_=grouped[:].rearrange("p n q j -> p (n q j)"))
+            return [(codes[:, n * Q:(n + 1) * Q], scales[:, n * Q:(n + 1) * Q]) for n in range(2)]
 
-        def gather(name, window, offsets, cols, dtype):
-            picked = sb.tile([P, cols], dtype, name=name, align_bytes=64)
+        def gather(name, window, offsets, cols, dtype, tag=""):
+            picked = sb.tile([P, cols], dtype, name=name, tag=tag or name, align_bytes=64)
             nc.vector.tensor_copy(out=picked[:], in_=window[:].indirect(offsets[:]))
             return picked
 
         def product(name, rows, words, scales, cols):
             acc = psum.tile([P, cols], F32, name=name)
-            nc.tensor.matmul_mx(out=acc[:], lhsT=rows[0][:].bitcast(FP8X4), lhsT_scale=rows[1][:],
+            nc.tensor.matmul_mx(out=acc[:], lhsT=rows[0].bitcast(FP8X4), lhsT_scale=rows[1],
                                 rhs=words[:].bitcast(FP4X4), rhs_scale=scales[:], start=True, stop=True)
             return acc
 
@@ -78,7 +75,7 @@ def tile_attend_hvevenmass_a_kernel(tc, pquery, pgsum_words, pgsum_scales, query
         val_words, val_scales = words_tile("val_words", T), scales_tile("val_scales", T)
         page_words, page_scales = words_tile("page_words", U), scales_tile("page_scales", U)
         nc.vector.memset(key_scales[:].bitcast(I32), 0)
-        nc.gpsimd.memset(val_scales[:].bitcast(I32), 0)
+        nc.vector.memset(val_scales[:].bitcast(I32), 0)
         nc.gpsimd.memset(page_scales[:].bitcast(I32), 0)
 
         nc.sync.dma_start(token_list[:], offs)
@@ -89,43 +86,42 @@ def tile_attend_hvevenmass_a_kernel(tc, pquery, pgsum_words, pgsum_scales, query
         load_words(val_words, vals_words)
         load_scales(val_scales, vals_scales)
         g_raw = load_rows("g", gout)
-        nc.sync.dma_start(page_list[:], offs2)
-        load_words(page_words, pgsum_words)
-        load_scales(page_scales, pgsum_scales)
         pq_raw = load_rows("pq", pquery)
+        load_words(page_words, pgsum_words)
+        nc.sync.dma_start(page_list[:], offs2)
+        load_scales(page_scales, pgsum_scales)
         even_t = sb.tile([P, 1], F32, name="even_t")
         nc.sync.dma_start(out=even_t[:], in_=even)
         base_t = sb.tile([P, I], F32, name="base_t")
         nc.sync.dma_start(out=base_t[:], in_=base)
 
-        q_bf = interleave("q", q_raw)
-        dq_bf = interleave("dq", dq_raw)
+        key_rows = sb.tile([P, 2, Q, PACK], BF16, name="key_rows", tag="key_rows", align_bytes=64)
+        interleave(key_rows[:, 0], q_raw)
+        interleave(key_rows[:, 1], dq_raw)
         kw = gather("kw", key_words, token_list, I, U16)
         ks = gather("ks", key_scales, token_list, I, U8)
-        q_mx = quantize("q", q_bf)
+        q_mx, dq_mx = quantize("key_rows", key_rows, ("key_rows_codes", "key_rows_scales"))
         a = product("a", q_mx, kw, ks, I)
-        dq_mx = quantize("dq", dq_bf)
         ta = product("ta", dq_mx, kw, ks, I)
         pa = sb.tile([P, I], F32, name="pa")
         nc.scalar.activation(out=pa[:], in_=a[:], func=ACT.Exp)
 
-        g_bf = interleave("g", g_raw)
-        pq_bf = interleave("pq", pq_raw)
-        vw = gather("vw", val_words, token_list, I, U16)
+        other_rows = sb.tile([P, 2, Q, PACK], BF16, name="other_rows", tag="other_rows", align_bytes=64)
+        interleave(other_rows[:, 0], g_raw)
+        interleave(other_rows[:, 1], pq_raw)
+        vw = gather("vw", val_words, token_list, I, U16, "key_rows")
         vs = gather("vs", val_scales, token_list, I, U8)
-        g_mx = quantize("g", g_bf)
-        c0 = product("c0", g_mx, vw, vs, I)
-
         pw = gather("pw", page_words, page_list, G, U16)
         ps = gather("ps", page_scales, page_list, G, U8)
-        pq_mx = quantize("pq", pq_bf)
+        g_mx, pq_mx = quantize("other_rows", other_rows, ("page_words", "page_scales"))
         b = product("b", pq_mx, pw, ps, G)
+        c0 = product("c0", g_mx, vw, vs, I)
 
-        def big(name):
-            return sb.tile([P, I], F32, name=name)
+        def big(name, tag=""):
+            return sb.tile([P, I], F32, name=name, tag=tag or name, align_bytes=64)
 
-        def small(name, cols=G):
-            return sb.tile([P, cols], F32, name=name)
+        def small(name, cols=G, tag=""):
+            return sb.tile([P, cols], F32, name=name, tag=tag or name, align_bytes=64)
 
         def paged(ap):
             return ap.rearrange("p (g r) -> p g r", r=R)
@@ -136,10 +132,12 @@ def tile_attend_hvevenmass_a_kernel(tc, pquery, pgsum_words, pgsum_scales, query
         def page_sum(dst, src):
             nc.vector.tensor_reduce(out=dst, in_=paged(src), axis=AX.X, op=ALU.add)
 
-        s = small("s")
+        s = small("s", G, "other_rows")
         page_sum(s[:], pa[:])
-        xpa = big("xpa")
+        xpa = big("xpa", "val_scales")
         nc.vector.tensor_tensor(out=xpa[:], in0=ta[:], in1=pa[:], op=ALU.mult)
+        rs = small("rs")
+        nc.vector.reciprocal(out=rs[:], in_=s[:])
         neg_max = small("neg_max", 1)
         nc.vector.tensor_reduce(out=neg_max[:], in_=b[:], axis=AX.X, op=ALU.max, negate=True)
         pb = small("pb")
@@ -149,16 +147,14 @@ def tile_attend_hvevenmass_a_kernel(tc, pquery, pgsum_words, pgsum_scales, query
         nc.scalar.activation(out=rest[:], in_=even_t[:], func=ACT.Copy, scale=-512.0, bias=512.0)
         floor = small("floor", 1)
         nc.scalar.activation(out=floor[:], in_=even_t[:], func=ACT.Copy, scale=512.0 / G)
-        rs = small("rs")
-        nc.vector.reciprocal(out=rs[:], in_=s[:])
         xs = small("xs")
         page_sum(xs[:], xpa[:])
-        rz = small("rz", 1)
-        nc.vector.reciprocal(out=rz[:], in_=zb[:])
         pc = big("pc")
         nc.vector.tensor_tensor(out=pc[:], in0=c0[:], in1=pa[:], op=ALU.mult)
         tbar = small("tbar")
         nc.vector.tensor_tensor(out=tbar[:], in0=xs[:], in1=rs[:], op=ALU.mult)
+        rz = small("rz", 1)
+        nc.vector.reciprocal(out=rz[:], in_=zb[:])
         share = small("share", 1)
         nc.scalar.activation(out=share[:], in_=rz[:], func=ACT.Copy, scale=rest[:])
         w = small("w")
@@ -171,23 +167,23 @@ def tile_attend_hvevenmass_a_kernel(tc, pquery, pgsum_words, pgsum_scales, query
         nc.vector.tensor_tensor(out=cbar[:], in0=pcs[:], in1=rs[:], op=ALU.mult)
         ws = small("ws")
         nc.vector.tensor_tensor(out=ws[:], in0=w[:], in1=rs[:], op=ALU.mult)
-        pu = big("pu")
-        nc.vector.tensor_tensor(out=pu[:], in0=pa[:], in1=u[:], op=ALU.mult)
         v = big("v")
         nc.vector.tensor_tensor(out=paged(v[:]), in0=paged(c0[:]), in1=spread(cbar[:]), op=ALU.subtract)
-        y = big("y")
-        nc.vector.tensor_tensor(out=paged(y[:]), in0=paged(pu[:]), in1=spread(ws[:]), op=ALU.mult)
+        pn = big("pn")
+        nc.vector.tensor_tensor(out=paged(pn[:]), in0=paged(pa[:]), in1=spread(ws[:]), op=ALU.mult)
 
-        yv, pcov, diff, res = big("yv"), big("pcov"), big("diff"), big("res")
+        z, yv, pcov, diff, res = big("z"), big("yv"), big("pcov"), big("diff"), big("res")
         dsum, cov = small("dsum"), small("cov")
         halves = [(slice(h * I // 2, (h + 1) * I // 2), slice(h * G // 2, (h + 1) * G // 2)) for h in range(2)]
         for cols, pages in halves:
-            nc.vector.tensor_tensor(out=yv[:, cols], in0=y[:, cols], in1=v[:, cols], op=ALU.mult)
+            nc.vector.tensor_tensor(out=z[:, cols], in0=u[:, cols], in1=v[:, cols], op=ALU.mult)
+        for cols, pages in halves:
+            nc.vector.tensor_tensor(out=yv[:, cols], in0=pn[:, cols], in1=z[:, cols], op=ALU.mult)
         for cols, pages in halves:
             page_sum(dsum[:, pages], yv[:, cols])
         for cols, pages in halves:
-            nc.vector.tensor_tensor(out=diff[:, cols], in0=yv[:, cols], in1=base_t[:, cols], op=ALU.add)
             nc.vector.tensor_tensor(out=cov[:, pages], in0=dsum[:, pages], in1=rs[:, pages], op=ALU.mult)
+            nc.vector.tensor_tensor(out=diff[:, cols], in0=yv[:, cols], in1=base_t[:, cols], op=ALU.add)
         for cols, pages in halves:
             nc.vector.tensor_tensor(out=paged(pcov[:, cols]), in0=paged(pa[:, cols]), in1=spread(cov[:, pages]), op=ALU.mult)
         for cols, pages in halves:

@@ -6,6 +6,7 @@ D, E, T, I, G, U, Q = 512, 512, 2048, 512, 64, 512, 128
 R = I // G
 P = 128
 PACK = 4
+GP = 48
 FLOPS = 2 * Q * (2 * D * I + E * I + D * G)
 
 F32 = mybir.dt.float32
@@ -27,6 +28,7 @@ def tile_attend_hvevenmass_a_kernel(tc, pquery, pgsum_words, pgsum_scales, query
     with ExitStack() as ctx:
         lists = ctx.enter_context(tc.tile_pool(name="lists", bufs=1))
         sb = ctx.enter_context(tc.tile_pool(name="sb", bufs=1))
+        shared = ctx.enter_context(tc.tile_pool(name="shared", bufs=1))
         psum = ctx.enter_context(tc.psum_pool(name="psum", bufs=1))
 
         token_list = lists.tile([P, I // 16], U16, name="token_list")
@@ -38,15 +40,15 @@ def tile_attend_hvevenmass_a_kernel(tc, pquery, pgsum_words, pgsum_scales, query
         def scales_tile(name, cols):
             return sb.tile([P, cols], U8, name=name, tag=name, align_bytes=64)
 
-        def load_words(tile, words):
-            nc.sync.dma_start(out=tile[:].bitcast(I32), in_=words[0].bitcast(I32))
+        def load_words(tile, words, queue):
+            queue.dma_start(out=tile[:].bitcast(I32), in_=words[0].bitcast(I32))
 
         def load_scales(tile, scales):
             for row in range(4):
                 nc.sync.dma_start(out=tile[row:P:32, :].bitcast(I32), in_=scales[0, row:16:4, :].bitcast(I32))
 
         def load_rows(name, rows):
-            raw = sb.tile([P, PACK, Q], F32, name=name + "_raw")
+            raw = sb.tile([P, PACK, Q], F32, name=name + "_raw", tag=name + "_raw")
             nc.sync.dma_start(out=raw[:], in_=rows.rearrange("(p j) q -> p j q", j=PACK))
             return raw
 
@@ -79,15 +81,15 @@ def tile_attend_hvevenmass_a_kernel(tc, pquery, pgsum_words, pgsum_scales, query
         nc.gpsimd.memset(page_scales[:].bitcast(I32), 0)
 
         nc.sync.dma_start(token_list[:], offs)
-        load_words(key_words, keys_words)
+        load_words(key_words, keys_words, nc.sync)
         load_scales(key_scales, keys_scales)
         q_raw = load_rows("q", query)
         dq_raw = load_rows("dq", dquery)
-        load_words(val_words, vals_words)
+        load_words(val_words, vals_words, nc.sync)
         load_scales(val_scales, vals_scales)
         g_raw = load_rows("g", gout)
         pq_raw = load_rows("pq", pquery)
-        load_words(page_words, pgsum_words)
+        load_words(page_words, pgsum_words, nc.sync)
         nc.sync.dma_start(page_list[:], offs2)
         load_scales(page_scales, pgsum_scales)
         even_t = sb.tile([P, 1], F32, name="even_t")
@@ -106,7 +108,7 @@ def tile_attend_hvevenmass_a_kernel(tc, pquery, pgsum_words, pgsum_scales, query
         pa = sb.tile([P, I], F32, name="pa")
         nc.scalar.activation(out=pa[:], in_=a[:], func=ACT.Exp)
 
-        other_rows = sb.tile([P, 2, Q, PACK], BF16, name="other_rows", tag="other_rows", align_bytes=64)
+        other_rows = shared.tile([P, 2, Q, PACK], BF16, name="other_rows", offset=0, align_bytes=64)
         interleave(other_rows[:, 0], g_raw)
         interleave(other_rows[:, 1], pq_raw)
         vw = gather("vw", val_words, token_list, I, U16, "key_rows")
@@ -132,12 +134,12 @@ def tile_attend_hvevenmass_a_kernel(tc, pquery, pgsum_words, pgsum_scales, query
         def page_sum(dst, src):
             nc.vector.tensor_reduce(out=dst, in_=paged(src), axis=AX.X, op=ALU.add)
 
-        s = small("s", G, "other_rows")
+        ta_sb = sb.tile([P, I], F32, name="ta_sb", tag="pq_raw")
+        nc.scalar.activation(out=ta_sb[:], in_=ta[:], func=ACT.Copy)
+        s = shared.tile([P, G], F32, name="s", offset=0, align_bytes=64)
         page_sum(s[:], pa[:])
-        xpa = big("xpa", "val_scales")
-        nc.vector.tensor_tensor(out=xpa[:], in0=ta[:], in1=pa[:], op=ALU.mult)
-        rs = small("rs")
-        nc.vector.reciprocal(out=rs[:], in_=s[:])
+        xpa = shared.tile([P, I], F32, name="xpa", offset=4 * G, align_bytes=64)
+        nc.gpsimd.tensor_tensor(out=xpa[:], in0=ta_sb[:], in1=pa[:], op=ALU.mult)
         neg_max = small("neg_max", 1)
         nc.vector.tensor_reduce(out=neg_max[:], in_=b[:], axis=AX.X, op=ALU.max, negate=True)
         pb = small("pb")
@@ -147,43 +149,45 @@ def tile_attend_hvevenmass_a_kernel(tc, pquery, pgsum_words, pgsum_scales, query
         nc.scalar.activation(out=rest[:], in_=even_t[:], func=ACT.Copy, scale=-512.0, bias=512.0)
         floor = small("floor", 1)
         nc.scalar.activation(out=floor[:], in_=even_t[:], func=ACT.Copy, scale=512.0 / G)
-        xs = small("xs")
-        page_sum(xs[:], xpa[:])
+        pbr = small("pbr")
+        nc.scalar.activation(out=pbr[:], in_=pb[:], func=ACT.Copy, scale=rest[:])
+        rs = small("rs")
+        nc.vector.reciprocal(out=rs[:], in_=s[:])
         pc = big("pc")
         nc.vector.tensor_tensor(out=pc[:], in0=c0[:], in1=pa[:], op=ALU.mult)
-        tbar = small("tbar")
-        nc.vector.tensor_tensor(out=tbar[:], in0=xs[:], in1=rs[:], op=ALU.mult)
         rz = small("rz", 1)
         nc.vector.reciprocal(out=rz[:], in_=zb[:])
-        share = small("share", 1)
-        nc.scalar.activation(out=share[:], in_=rz[:], func=ACT.Copy, scale=rest[:])
-        w = small("w")
-        nc.scalar.activation(out=w[:], in_=pb[:], func=ACT.Identity, scale=share[:], bias=floor[:])
-        pcs = small("pcs")
+        sums = small("sums", 2 * G)
+        nc.scalar.activation(out=sums[:, G:], in_=pbr[:], func=ACT.Identity, scale=rz[:], bias=floor[:])
+        page_sum(sums[:, :G], xpa[:])
+        pcs = small("pcs", G, "zb")
         page_sum(pcs[:], pc[:])
-        u = big("u")
-        nc.vector.tensor_tensor(out=paged(u[:]), in0=paged(ta[:]), in1=spread(tbar[:]), op=ALU.subtract)
+        means = small("means", 2 * G)
+        nc.vector.tensor_tensor(out=means[:].rearrange("p (n g) -> p n g", n=2), in0=sums[:].rearrange("p (n g) -> p n g", n=2),
+                                in1=rs[:].unsqueeze(1).to_broadcast([P, 2, G]), op=ALU.mult)
         cbar = small("cbar")
         nc.vector.tensor_tensor(out=cbar[:], in0=pcs[:], in1=rs[:], op=ALU.mult)
-        ws = small("ws")
-        nc.vector.tensor_tensor(out=ws[:], in0=w[:], in1=rs[:], op=ALU.mult)
+        tbar, ws = means[:, :G], means[:, G:]
+        halves = [(slice(h * I // 2, (h + 1) * I // 2), slice(h * G // 2, (h + 1) * G // 2)) for h in range(2)]
+        pn = big("pn", "zb")
+        nc.gpsimd.tensor_tensor(out=paged(pn[:, :R * GP]), in0=paged(pa[:, :R * GP]), in1=spread(ws[:, :GP]), op=ALU.mult)
+        u = big("u")
+        nc.vector.tensor_tensor(out=paged(u[:]), in0=paged(ta[:]), in1=spread(tbar), op=ALU.subtract)
         v = big("v")
         nc.vector.tensor_tensor(out=paged(v[:]), in0=paged(c0[:]), in1=spread(cbar[:]), op=ALU.subtract)
-        pn = big("pn")
-        nc.vector.tensor_tensor(out=paged(pn[:]), in0=paged(pa[:]), in1=spread(ws[:]), op=ALU.mult)
+        nc.vector.tensor_tensor(out=paged(pn[:, R * GP:]), in0=paged(pa[:, R * GP:]), in1=spread(ws[:, GP:]), op=ALU.mult)
 
         z, yv, pcov, diff, res = big("z"), big("yv"), big("pcov"), big("diff"), big("res")
         dsum, cov = small("dsum"), small("cov")
-        halves = [(slice(h * I // 2, (h + 1) * I // 2), slice(h * G // 2, (h + 1) * G // 2)) for h in range(2)]
         for cols, pages in halves:
             nc.vector.tensor_tensor(out=z[:, cols], in0=u[:, cols], in1=v[:, cols], op=ALU.mult)
         for cols, pages in halves:
             nc.vector.tensor_tensor(out=yv[:, cols], in0=pn[:, cols], in1=z[:, cols], op=ALU.mult)
         for cols, pages in halves:
             page_sum(dsum[:, pages], yv[:, cols])
-        for cols, pages in halves:
+        for adder, (cols, pages) in zip((nc.vector, nc.gpsimd), halves):
             nc.vector.tensor_tensor(out=cov[:, pages], in0=dsum[:, pages], in1=rs[:, pages], op=ALU.mult)
-            nc.vector.tensor_tensor(out=diff[:, cols], in0=yv[:, cols], in1=base_t[:, cols], op=ALU.add)
+            adder.tensor_tensor(out=diff[:, cols], in0=yv[:, cols], in1=base_t[:, cols], op=ALU.add)
         for cols, pages in halves:
             nc.vector.tensor_tensor(out=paged(pcov[:, cols]), in0=paged(pa[:, cols]), in1=spread(cov[:, pages]), op=ALU.mult)
         for cols, pages in halves:

@@ -43,21 +43,20 @@ def tile_attend_hvevenmass_a_kernel(tc, pquery, pgsum_words, pgsum_scales, query
         def load_words(tile, words, queue):
             queue.dma_start(out=tile[:].bitcast(I32), in_=words[0].bitcast(I32))
 
-        def load_scales(tile, scales):
+        def load_scales(tile, scales, queue):
             for row in range(4):
-                nc.sync.dma_start(out=tile[row:P:32, :].bitcast(I32), in_=scales[0, row:16:4, :].bitcast(I32))
+                queue.dma_start(out=tile[row:P:32, :].bitcast(I32), in_=scales[0, row:16:4, :].bitcast(I32))
 
-        def load_rows(name, rows):
-            raw = sb.tile([P, PACK, Q], F32, name=name + "_raw", tag=name + "_raw")
+        def load_rows(raw, rows):
             nc.sync.dma_start(out=raw[:], in_=rows.rearrange("(p j) q -> p j q", j=PACK))
             return raw
 
         def interleave(grouped, raw):
             nc.scalar.activation(out=grouped, in_=raw[:].rearrange("p j q -> p q j"), func=ACT.Copy)
 
-        def quantize(name, grouped, tags):
-            codes = sb.tile([P, 2 * Q], U32, name=name + "_codes", tag=tags[0], align_bytes=64)
-            scales = sb.tile([P, 2 * Q], U8, name=name + "_scales", tag=tags[1], align_bytes=64)
+        def quantize(name, grouped):
+            codes = sb.tile([P, 2 * Q], U32, name=name + "_codes", align_bytes=64)
+            scales = sb.tile([P, 2 * Q], U8, name=name + "_scales", align_bytes=64)
             nc.vector.quantize_mx(out=codes[:].bitcast(FP8X4), scales=scales[:],
                                   in_=grouped[:].rearrange("p n q j -> p (n q j)"))
             return [(codes[:, n * Q:(n + 1) * Q], scales[:, n * Q:(n + 1) * Q]) for n in range(2)]
@@ -80,44 +79,43 @@ def tile_attend_hvevenmass_a_kernel(tc, pquery, pgsum_words, pgsum_scales, query
         nc.vector.memset(val_scales[:].bitcast(I32), 0)
         nc.gpsimd.memset(page_scales[:].bitcast(I32), 0)
 
-        nc.sync.dma_start(token_list[:], offs)
         load_words(key_words, keys_words, nc.sync)
-        load_scales(key_scales, keys_scales)
-        q_raw = load_rows("q", query)
-        dq_raw = load_rows("dq", dquery)
+        nc.sync.dma_start(token_list[:], offs)
+        load_scales(key_scales, keys_scales, nc.sync)
+        load_scales(page_scales, pgsum_scales, nc.gpsimd)
+        q_raw = load_rows(sb.tile([P, PACK, Q], F32, name="q_raw"), query)
         load_words(val_words, vals_words, nc.sync)
-        load_scales(val_scales, vals_scales)
-        g_raw = load_rows("g", gout)
-        pq_raw = load_rows("pq", pquery)
+        dq_raw = load_rows(sb.tile([P, PACK, Q], F32, name="dq_raw"), dquery)
+        load_scales(val_scales, vals_scales, nc.sync)
+        g_raw = load_rows(sb.tile([P, PACK, Q], F32, name="g_raw"), gout)
+        pq_raw = load_rows(shared.tile([P, PACK, Q], F32, name="pq_raw", offset=2 * I), pquery)
         load_words(page_words, pgsum_words, nc.sync)
         nc.sync.dma_start(page_list[:], offs2)
-        load_scales(page_scales, pgsum_scales)
         even_t = sb.tile([P, 1], F32, name="even_t")
         nc.sync.dma_start(out=even_t[:], in_=even)
         base_t = sb.tile([P, I], F32, name="base_t")
         nc.sync.dma_start(out=base_t[:], in_=base)
 
-        key_rows = sb.tile([P, 2, Q, PACK], BF16, name="key_rows", tag="key_rows", align_bytes=64)
+        key_rows = sb.tile([P, 2, Q, PACK], BF16, name="key_rows", align_bytes=64)
         interleave(key_rows[:, 0], q_raw)
         interleave(key_rows[:, 1], dq_raw)
-        kw = gather("kw", key_words, token_list, I, U16)
-        ks = gather("ks", key_scales, token_list, I, U8)
-        q_mx, dq_mx = quantize("key_rows", key_rows, ("key_rows_codes", "key_rows_scales"))
-        a = product("a", q_mx, kw, ks, I)
-        ta = product("ta", dq_mx, kw, ks, I)
-        pa = sb.tile([P, I], F32, name="pa")
-        nc.scalar.activation(out=pa[:], in_=a[:], func=ACT.Exp)
-
-        other_rows = shared.tile([P, 2, Q, PACK], BF16, name="other_rows", offset=0, align_bytes=64)
+        other_rows = sb.tile([P, 2, Q, PACK], BF16, name="other_rows", tag="other_rows", align_bytes=64)
         interleave(other_rows[:, 0], g_raw)
         interleave(other_rows[:, 1], pq_raw)
-        vw = gather("vw", val_words, token_list, I, U16, "key_rows")
+        kw = gather("kw", key_words, token_list, I, U16)
+        ks = gather("ks", key_scales, token_list, I, U8)
+        vw = gather("vw", val_words, token_list, I, U16)
+        q_mx, dq_mx = quantize("key_rows", key_rows)
+        a = product("a", q_mx, kw, ks, I)
+        ta = product("ta", dq_mx, kw, ks, I)
+        pa = shared.tile([P, I], F32, name="pa", offset=0)
+        nc.scalar.activation(out=pa[:], in_=a[:], func=ACT.Exp)
         vs = gather("vs", val_scales, token_list, I, U8)
+        g_mx, pq_mx = quantize("other_rows", other_rows)
+        c0 = product("c0", g_mx, vw, vs, I)
         pw = gather("pw", page_words, page_list, G, U16)
         ps = gather("ps", page_scales, page_list, G, U8)
-        g_mx, pq_mx = quantize("other_rows", other_rows, ("page_words", "page_scales"))
         b = product("b", pq_mx, pw, ps, G)
-        c0 = product("c0", g_mx, vw, vs, I)
 
         def big(name, tag=""):
             return sb.tile([P, I], F32, name=name, tag=tag or name, align_bytes=64)
@@ -134,11 +132,11 @@ def tile_attend_hvevenmass_a_kernel(tc, pquery, pgsum_words, pgsum_scales, query
         def page_sum(dst, src):
             nc.vector.tensor_reduce(out=dst, in_=paged(src), axis=AX.X, op=ALU.add)
 
-        ta_sb = sb.tile([P, I], F32, name="ta_sb", tag="pq_raw")
+        ta_sb = shared.tile([P, I], F32, name="ta_sb", offset=4 * I)
         nc.scalar.activation(out=ta_sb[:], in_=ta[:], func=ACT.Copy)
-        s = shared.tile([P, G], F32, name="s", offset=0, align_bytes=64)
+        s = small("s", G, "page_words")
         page_sum(s[:], pa[:])
-        xpa = shared.tile([P, I], F32, name="xpa", offset=4 * G, align_bytes=64)
+        xpa = big("xpa", "other_rows")
         nc.gpsimd.tensor_tensor(out=xpa[:], in0=ta_sb[:], in1=pa[:], op=ALU.mult)
         neg_max = small("neg_max", 1)
         nc.vector.tensor_reduce(out=neg_max[:], in_=b[:], axis=AX.X, op=ALU.max, negate=True)

from contextlib import ExitStack

import concourse.mybir as mybir

D, E, T, I, G, U, Q = 512, 512, 2048, 512, 64, 512, 128
R = I // G
P = 128
PACK = 4
GP = 48
FLOPS = 2 * Q * (2 * D * I + E * I + D * G)

F32 = mybir.dt.float32
BF16 = mybir.dt.bfloat16
I32 = mybir.dt.int32
U32 = mybir.dt.uint32
U16 = mybir.dt.uint16
U8 = mybir.dt.uint8
FP8X4 = mybir.dt.float8_e4m3fn_x4
FP4X4 = mybir.dt.float4_e2m1fn_x4
ALU = mybir.AluOpType
ACT = mybir.ActivationFunctionType
AX = mybir.AxisListType


def tile_attend_hvevenmass_a_kernel(tc, pquery, pgsum_words, pgsum_scales, query, keys_words, keys_scales, even, gout,
                                     vals_words, vals_scales, dquery, base, offs, offs2, out):
    nc = tc.nc
    with ExitStack() as ctx:
        lists = ctx.enter_context(tc.tile_pool(name="lists", bufs=1))
        sb = ctx.enter_context(tc.tile_pool(name="sb", bufs=1))
        shared = ctx.enter_context(tc.tile_pool(name="shared", bufs=1))
        psum = ctx.enter_context(tc.psum_pool(name="psum", bufs=1))

        token_list = lists.tile([P, I // 16], U16, name="token_list")
        page_list = lists.tile([P, G // 16], U16, name="page_list")

        def words_tile(name, cols):
            return sb.tile([P, cols], U16, name=name, tag=name, align_bytes=64)

        def scales_tile(name, cols):
            return sb.tile([P, cols], U8, name=name, tag=name, align_bytes=64)

        def load_words(tile, words, queue):
            queue.dma_start(out=tile[:].bitcast(I32), in_=words[0].bitcast(I32))

        def load_scales(tile, scales, queue):
            for row in range(4):
                queue.dma_start(out=tile[row:P:32, :].bitcast(I32), in_=scales[0, row:16:4, :].bitcast(I32))

        def load_rows(raw, rows):
            nc.sync.dma_start(out=raw[:], in_=rows.rearrange("(p j) q -> p j q", j=PACK))
            return raw

        def interleave(grouped, raw):
            nc.scalar.activation(out=grouped, in_=raw[:].rearrange("p j q -> p q j"), func=ACT.Copy)

        def quantize(name, grouped):
            codes = sb.tile([P, 2 * Q], U32, name=name + "_codes", align_bytes=64)
            scales = sb.tile([P, 2 * Q], U8, name=name + "_scales", align_bytes=64)
            nc.vector.quantize_mx(out=codes[:].bitcast(FP8X4), scales=scales[:],
                                  in_=grouped[:].rearrange("p n q j -> p (n q j)"))
            return [(codes[:, n * Q:(n + 1) * Q], scales[:, n * Q:(n + 1) * Q]) for n in range(2)]

        def gather(name, window, offsets, cols, dtype, tag=""):
            picked = sb.tile([P, cols], dtype, name=name, tag=tag or name, align_bytes=64)
            nc.vector.tensor_copy(out=picked[:], in_=window[:].indirect(offsets[:]))
            return picked

        def product(name, rows, words, scales, cols):
            acc = psum.tile([P, cols], F32, name=name)
            nc.tensor.matmul_mx(out=acc[:], lhsT=rows[0].bitcast(FP8X4), lhsT_scale=rows[1],
                                rhs=words[:].bitcast(FP4X4), rhs_scale=scales[:], start=True, stop=True)
            return acc

        key_words, key_scales = words_tile("key_words", T), scales_tile("key_scales", T)
        val_words, val_scales = words_tile("val_words", T), scales_tile("val_scales", T)
        page_words, page_scales = words_tile("page_words", U), scales_tile("page_scales", U)
        nc.vector.memset(key_scales[:].bitcast(I32), 0)
        nc.vector.memset(val_scales[:].bitcast(I32), 0)
        nc.gpsimd.memset(page_scales[:].bitcast(I32), 0)

        load_words(key_words, keys_words, nc.sync)
        nc.sync.dma_start(token_list[:], offs)
        load_scales(key_scales, keys_scales, nc.sync)
        load_scales(page_scales, pgsum_scales, nc.gpsimd)
        q_raw = load_rows(sb.tile([P, PACK, Q], F32, name="q_raw"), query)
        load_words(val_words, vals_words, nc.sync)
        dq_raw = load_rows(sb.tile([P, PACK, Q], F32, name="dq_raw"), dquery)
        load_scales(val_scales, vals_scales, nc.sync)
        g_raw = load_rows(sb.tile([P, PACK, Q], F32, name="g_raw"), gout)
        pq_raw = load_rows(shared.tile([P, PACK, Q], F32, name="pq_raw", offset=2 * I), pquery)
        load_words(page_words, pgsum_words, nc.sync)
        nc.sync.dma_start(page_list[:], offs2)
        even_t = sb.tile([P, 1], F32, name="even_t")
        nc.sync.dma_start(out=even_t[:], in_=even)
        base_t = sb.tile([P, I], F32, name="base_t")
        nc.sync.dma_start(out=base_t[:], in_=base)

        key_rows = sb.tile([P, 2, Q, PACK], BF16, name="key_rows", align_bytes=64)
        interleave(key_rows[:, 0], q_raw)
        interleave(key_rows[:, 1], dq_raw)
        other_rows = sb.tile([P, 2, Q, PACK], BF16, name="other_rows", tag="other_rows", align_bytes=64)
        interleave(other_rows[:, 0], g_raw)
        interleave(other_rows[:, 1], pq_raw)
        kw = gather("kw", key_words, token_list, I, U16)
        ks = gather("ks", key_scales, token_list, I, U8)
        vw = gather("vw", val_words, token_list, I, U16)
        q_mx, dq_mx = quantize("key_rows", key_rows)
        a = product("a", q_mx, kw, ks, I)
        ta = product("ta", dq_mx, kw, ks, I)
        pa = shared.tile([P, I], F32, name="pa", offset=0)
        nc.scalar.activation(out=pa[:], in_=a[:], func=ACT.Exp)
        vs = gather("vs", val_scales, token_list, I, U8)
        g_mx, pq_mx = quantize("other_rows", other_rows)
        c0 = product("c0", g_mx, vw, vs, I)
        pw = gather("pw", page_words, page_list, G, U16)
        ps = gather("ps", page_scales, page_list, G, U8)
        b = product("b", pq_mx, pw, ps, G)

        def big(name, tag=""):
            return sb.tile([P, I], F32, name=name, tag=tag or name, align_bytes=64)

        def small(name, cols=G, tag=""):
            return sb.tile([P, cols], F32, name=name, tag=tag or name, align_bytes=64)

        def paged(ap):
            return ap.rearrange("p (g r) -> p g r", r=R)

        def spread(ap):
            return ap.unsqueeze(2).to_broadcast([P, ap.shape[1], R])

        def page_sum(dst, src):
            nc.vector.tensor_reduce(out=dst, in_=paged(src), axis=AX.X, op=ALU.add)

        ta_sb = shared.tile([P, I], F32, name="ta_sb", offset=4 * I)
        nc.scalar.activation(out=ta_sb[:], in_=ta[:], func=ACT.Copy)
        s = small("s", G, "page_words")
        page_sum(s[:], pa[:])
        xpa = big("xpa", "other_rows")
        nc.gpsimd.tensor_tensor(out=xpa[:], in0=ta_sb[:], in1=pa[:], op=ALU.mult)
        neg_max = small("neg_max", 1)
        nc.vector.tensor_reduce(out=neg_max[:], in_=b[:], axis=AX.X, op=ALU.max, negate=True)
        pb = small("pb")
        zb = small("zb", 1)
        nc.scalar.activation(out=pb[:], in_=b[:], func=ACT.Exp, bias=neg_max[:], accum_out=zb[:])
        rest = small("rest", 1)
        nc.scalar.activation(out=rest[:], in_=even_t[:], func=ACT.Copy, scale=-512.0, bias=512.0)
        floor = small("floor", 1)
        nc.scalar.activation(out=floor[:], in_=even_t[:], func=ACT.Copy, scale=512.0 / G)
        pbr = small("pbr")
        nc.scalar.activation(out=pbr[:], in_=pb[:], func=ACT.Copy, scale=rest[:])
        rs = small("rs")
        nc.vector.reciprocal(out=rs[:], in_=s[:])
        pc = big("pc")
        nc.vector.tensor_tensor(out=pc[:], in0=c0[:], in1=pa[:], op=ALU.mult)
        rz = small("rz", 1)
        nc.vector.reciprocal(out=rz[:], in_=zb[:])
        sums = small("sums", 2 * G)
        nc.scalar.activation(out=sums[:, G:], in_=pbr[:], func=ACT.Identity, scale=rz[:], bias=floor[:])
        page_sum(sums[:, :G], xpa[:])
        pcs = small("pcs", G, "zb")
        page_sum(pcs[:], pc[:])
        means = small("means", 2 * G)
        nc.vector.tensor_tensor(out=means[:].rearrange("p (n g) -> p n g", n=2), in0=sums[:].rearrange("p (n g) -> p n g", n=2),
                                in1=rs[:].unsqueeze(1).to_broadcast([P, 2, G]), op=ALU.mult)
        cbar = small("cbar")
        nc.vector.tensor_tensor(out=cbar[:], in0=pcs[:], in1=rs[:], op=ALU.mult)
        tbar, ws = means[:, :G], means[:, G:]
        halves = [(slice(h * I // 2, (h + 1) * I // 2), slice(h * G // 2, (h + 1) * G // 2)) for h in range(2)]
        pn = big("pn", "zb")
        nc.gpsimd.tensor_tensor(out=paged(pn[:, :R * GP]), in0=paged(pa[:, :R * GP]), in1=spread(ws[:, :GP]), op=ALU.mult)
        u = big("u")
        nc.vector.tensor_tensor(out=paged(u[:]), in0=paged(ta[:]), in1=spread(tbar), op=ALU.subtract)
        v = big("v")
        nc.vector.tensor_tensor(out=paged(v[:]), in0=paged(c0[:]), in1=spread(cbar[:]), op=ALU.subtract)
        nc.vector.tensor_tensor(out=paged(pn[:, R * GP:]), in0=paged(pa[:, R * GP:]), in1=spread(ws[:, GP:]), op=ALU.mult)

        z, yv, pcov, diff, res = big("z"), big("yv"), big("pcov"), big("diff"), big("res")
        dsum, cov = small("dsum"), small("cov")
        for cols, pages in halves:
            nc.vector.tensor_tensor(out=z[:, cols], in0=u[:, cols], in1=v[:, cols], op=ALU.mult)
        for cols, pages in halves:
            nc.vector.tensor_tensor(out=yv[:, cols], in0=pn[:, cols], in1=z[:, cols], op=ALU.mult)
        for cols, pages in halves:
            page_sum(dsum[:, pages], yv[:, cols])
        for adder, (cols, pages) in zip((nc.vector, nc.gpsimd), halves):
            nc.vector.tensor_tensor(out=cov[:, pages], in0=dsum[:, pages], in1=rs[:, pages], op=ALU.mult)
            adder.tensor_tensor(out=diff[:, cols], in0=yv[:, cols], in1=base_t[:, cols], op=ALU.add)
        for cols, pages in halves:
            nc.vector.tensor_tensor(out=paged(pcov[:, cols]), in0=paged(pa[:, cols]), in1=spread(cov[:, pages]), op=ALU.mult)
        for cols, pages in halves:
            nc.vector.tensor_tensor(out=res[:, cols], in0=diff[:, cols], in1=pcov[:, cols], op=ALU.subtract)
            nc.sync.dma_start(out=out[:, cols], in_=res[:, cols])
